import numpy as np
import ml_dtypes


def mxq(x, axis, fmt="e4m3"):
    dtype, down = {"e4m3": (ml_dtypes.float8_e4m3fn, 7), "e5m2": (ml_dtypes.float8_e5m2, 14)}[fmt]
    v = np.moveaxis(np.asarray(x, np.float32).astype(ml_dtypes.bfloat16).astype(np.float64), axis, -1)
    blocks = v.reshape(v.shape[:-1] + (-1, 32))
    amax = np.abs(blocks).max(-1, keepdims=True)
    byte = np.maximum(np.where(amax > 0, np.frexp(amax)[1] - 1 + 127, 0) - down, 1)
    scale = np.exp2(byte - 127.0)
    codes = (blocks / scale).astype(np.float32).astype(dtype).astype(np.float64)
    return np.moveaxis((codes * scale).reshape(v.shape), -1, axis)


WIDE = False


def mx_kscale(k):
    if not WIDE:
        return np.ones(k)
    levels = np.array([10, -10, 5, -5, 0])
    if k % 512:
        return np.exp2(np.random.permutation(np.resize(levels, k // 32))).repeat(32)
    a = np.empty((k // 512, 16))
    for p in range(k // 512):
        a[p, :8] = np.random.permutation(np.resize(levels, 8))
        for g in range(8):
            far = levels[np.abs(levels - a[p, g]) >= 10]
            a[p, g + 8] = far[np.random.randint(len(far))]
    return np.exp2(a.ravel()).repeat(32)


def f64(x):
    return np.asarray(x).astype(np.float64)


def striped(idx):
    return np.tile(idx.reshape(-1, 16).T, (8, 1)).astype(np.uint16)


def unstriped(offs):
    return offs[:16].T.reshape(-1).astype(np.int64)


E2M1 = np.array([0.0, 0.5, 1.0, 1.5, 2.0, 3.0, 4.0, 6.0, -0.0, -0.5, -1.0, -1.5, -2.0, -3.0, -4.0, -6.0])


def pack_weight(w, fmt):
    k, n = w.shape
    w = f64(np.asarray(w, np.float32).astype(ml_dtypes.bfloat16)).reshape(k // 32, 32, n)
    amax = np.abs(w).max(1)
    if fmt == "e4m3":
        byte = np.frexp(amax)[1] - 1 + 127 - 7
    else:
        mant, ex = np.frexp(amax / 6.0)
        byte = np.where(mant > 0.5, ex, ex - 1) + 127
    byte = np.clip(np.where(amax > 0, byte, 1), 1, 254)
    scaled = (w * np.exp2(127.0 - byte)[:, None, :]).reshape(k, n).astype(np.float32)
    by_word = np.ascontiguousarray(scaled.reshape(k // 512, 128, 4, n).transpose(0, 1, 3, 2))
    if fmt == "e4m3":
        words = by_word.astype(ml_dtypes.float8_e4m3fn).view(np.uint8)
    else:
        c = by_word.astype(ml_dtypes.float4_e2m1fn).view(np.uint8) & 0xF
        words = (c[..., 0::2] | (c[..., 1::2] << 4)).reshape(k // 512, 128, 2 * n)
    return np.ascontiguousarray(words), np.ascontiguousarray(byte.astype(np.uint8).reshape(k // 512, 16, n))


def unpack_weight(words, scales, fmt):
    g, _, n = scales.shape
    words = np.ascontiguousarray(words).reshape(g, 128, n, -1)
    if fmt == "e4m3":
        vals = words.view(ml_dtypes.float8_e4m3fn).astype(np.float64)
    else:
        nib = np.empty((g, 128, n, 4), np.uint8)
        nib[..., 0::2] = words & 0xF
        nib[..., 1::2] = words >> 4
        vals = E2M1[nib]
    vals = vals * np.repeat(np.exp2(scales.astype(np.float64) - 127.0), 8, axis=1)[..., None]
    return vals.transpose(0, 1, 3, 2).reshape(g * 512, n)


def gelu(v):
    return 0.5 * v * (1.0 + np.tanh(np.sqrt(2.0 / np.pi) * (v + 0.044715 * v**3)))


K, KA, T, S, H, T3, S2 = 1536, 1024, 2048, 512, 1024, 2048, 512


def setup_inputs():
    n = np.random.standard_normal
    s = mx_kscale(K)[:, None]
    u = mx_kscale(H)[:, None]
    tab_words, tab_scales = pack_weight(n((K, T)) * s, "e4m3")
    tab2_words, tab2_scales = pack_weight(n((H, T3)) / u / np.sqrt(H), "e4m3")
    tab3_words, tab3_scales = pack_weight(n((H, T3)) / u / np.sqrt(H), "e4m3")
    w4_words, w4_scales = pack_weight(n((KA, H)) / s[:KA] / np.sqrt(K), "e2m1")
    return {
        "tab_words": tab_words, "tab_scales": tab_scales,
        "offs": striped(np.random.permutation(T)[:S]),
        "tab2_words": tab2_words, "tab2_scales": tab2_scales,
        "offs2": striped(np.random.permutation(T3)[:S2]),
        "tab3_words": tab3_words, "tab3_scales": tab3_scales,
        "offs3": striped(np.random.permutation(T3)[:S2]),
        "w4_words": w4_words, "w4_scales": w4_scales,
        "w1": (n((K - KA, H)) / s[KA:] / np.sqrt(K)).astype(np.float32),
        "b": (0.7 * n(H)).astype(np.float32),
        "gain": (0.45 * np.exp(0.3 * n(H)) * u[:, 0]).astype(np.float32),
        "wrow": np.exp(0.4 * n(S2)).astype(np.float32),
    }


def reference(tab_words, tab_scales, offs, tab2_words, tab2_scales, offs2, tab3_words, tab3_scales, offs3,
              w4_words, w4_scales, w1, b, gain, wrow):
    v = unpack_weight(tab_words, tab_scales, "e4m3")[:, unstriped(offs)]
    v2 = unpack_weight(tab2_words, tab2_scales, "e4m3")[:, unstriped(offs2)]
    v3 = unpack_weight(tab3_words, tab3_scales, "e4m3")[:, unstriped(offs3)]
    w4 = unpack_weight(w4_words, w4_scales, "e2m1")
    wq = mxq(f64(w1), 0, "e4m3")
    x = w4.T @ v[:KA] + wq.T @ v[KA:]
    h = f64(gain)[:, None] * np.abs(x + f64(b)[:, None])
    hq = mxq(h, 0, "e4m3")
    e2 = v2.T @ hq
    e3 = v3.T @ hq
    best = np.maximum(np.sin(e2) * e3, e3)
    return f64(wrow)[:, None] * best

@@ -1,0 +1,261 @@
+import math
+from contextlib import ExitStack
+
+import concourse.mybir as mybir
+
+K, KA, T, S, H, S2 = 1536, 1024, 2048, 512, 1024, 512
+FLOPS = 2 * K * H * S + 2 * 2 * H * S2 * S
+
+F32 = mybir.dt.float32
+BF16 = mybir.dt.bfloat16
+I32 = mybir.dt.int32
+U32 = mybir.dt.uint32
+U16 = mybir.dt.uint16
+U8 = mybir.dt.uint8
+FP8X4 = mybir.dt.float8_e4m3fn_x4
+FP4X4 = mybir.dt.float4_e2m1fn_x4
+ALU = mybir.AluOpType
+ACT = mybir.ActivationFunctionType
+
+P = 128
+HALF = 256
+LIST_COLS = S // 16
+ROUNDER = 1.5 * 2.0**23
+
+
+def tile_list_islet_batch_scores_kernel(
+    tc, tab_words, tab_scales, offs, tab2_words, tab2_scales, offs2, tab3_words, tab3_scales, offs3,
+    w4_words, w4_scales, w1, b, gain, wrow, out,
+):
+    nc = tc.nc
+    with ExitStack() as ctx:
+        keep = ctx.enter_context(tc.tile_pool(name="keep", bufs=1))
+        psum = ctx.enter_context(tc.psum_pool(name="psum", bufs=1))
+
+        def sb(name, shape, dtype):
+            return keep.tile(shape, dtype, name=name, align_bytes=64)
+
+        list1 = keep.tile([P, LIST_COLS], U16, name="list1")
+        list2 = keep.tile([P, LIST_COLS], U16, name="list2")
+        list3 = keep.tile([P, LIST_COLS], U16, name="list3")
+
+        w4_sc = sb("w4_sc", [P, 2, H], U8)
+        v_sc = sb("v_sc", [P, 2, T], U8)
+        v2_sc = sb("v2_sc", [P, T], U8)
+        v3_sc = sb("v3_sc", [P, T], U8)
+        for plane in (w4_sc, v_sc, v2_sc, v3_sc):
+            nc.vector.memset(plane[:].bitcast(I32), 0)
+
+        def load_words(name, words):
+            tile = sb(name, [P, T], U32)
+            nc.sync.dma_start(tile[:].bitcast(I32), words.rearrange("p n t -> p (n t)").bitcast(I32))
+            return tile
+
+        def load_w1(h):
+            tile = sb("w1_raw%d" % h, [P, 4, 512], F32)
+            nc.sync.dma_start(tile[:], w1[:, 512 * h : 512 * (h + 1)].rearrange("(p j) c -> p j c", j=4))
+            return tile
+
+        nc.sync.dma_start(list1[:], offs)
+        for q in range(4):
+            nc.scalar.dma_start(
+                w4_sc[32 * q : 32 * q + 4, :, :].bitcast(I32),
+                w4_scales[:, 4 * q : 4 * q + 4, :].rearrange("a r n -> r a n").bitcast(I32),
+            )
+        w4_raw = sb("w4_raw", [P, 2, 2 * H], U8)
+        nc.sync.dma_start(w4_raw[:].bitcast(I32), w4_words.rearrange("a p n -> p a n").bitcast(I32))
+        v_words = [load_words("v_words0", tab_words[0])]
+        w1_raw = [load_w1(0)]
+        for q in range(4):
+            nc.scalar.dma_start(
+                v_sc[32 * q : 32 * q + 4, :, :].bitcast(I32),
+                tab_scales[0:2, 4 * q : 4 * q + 4, :].rearrange("a r n -> r a n").bitcast(I32),
+            )
+        w1_raw.append(load_w1(1))
+        v_words.append(load_words("v_words1", tab_words[1]))
+        v_words.append(load_words("v_words2", tab_words[2]))
+        b_sb = sb("b_sb", [P, 2, 4], F32)
+        g_sb = sb("g_sb", [P, 2, 4], F32)
+        w_sb = sb("w_sb", [P, 4], F32)
+        nc.sync.dma_start(b_sb[:], b.rearrange("(h p t) -> p h t", h=2, t=4))
+        nc.sync.dma_start(g_sb[:], gain.rearrange("(h p t) -> p h t", h=2, t=4))
+        nc.sync.dma_start(list2[:], offs2)
+        nc.sync.dma_start(list3[:], offs3)
+        with nc.allow_non_contiguous_dma(reason="one row weight a partition"):
+            nc.sync.dma_start(w_sb[:], wrow.rearrange("(c p) -> p c", p=P))
+        v2_words = [load_words("v2_words%d" % a, tab2_words[a]) for a in range(2)]
+        v3_words = [load_words("v3_words%d" % a, tab3_words[a]) for a in range(2)]
+
+        V_K, V2_K, V3_K = 4, 8, 4
+        for q in range(4):
+            nc.gpsimd.dma_start(
+                v_sc[32 * q + V_K : 32 * q + V_K + 4, 1, :].bitcast(I32),
+                tab_scales[2, 4 * q : 4 * q + 4, :].bitcast(I32),
+            )
+        for plane, scales, k in ((v2_sc, tab2_scales, V2_K), (v3_sc, tab3_scales, V3_K)):
+            for q in range(4):
+                nc.gpsimd.dma_start(
+                    plane[32 * q + k : 32 * q + k + 8, :].bitcast(I32),
+                    scales[:, 4 * q : 4 * q + 4, :].bitcast(I32),
+                )
+
+        w4_deal = sb("w4_deal", [P, 2, 2 * H], U8)
+        w4_sc_deal = sb("w4_sc_deal", [P, 2, H], U8)
+        nc.vector.tensor_copy(
+            w4_deal[:].bitcast(U16).rearrange("p a (h t m) -> p (a h) t m", h=2, t=4),
+            w4_raw[:].bitcast(U16).rearrange("p a (h m t) -> p (a h) t m", h=2, t=4),
+        )
+        nc.vector.tensor_copy(
+            w4_sc_deal[:].rearrange("p a (h t m) -> p (a h) t m", h=2, t=4),
+            w4_sc[:].rearrange("p a (h m t) -> p (a h) t m", h=2, t=4),
+        )
+
+        def gather(dst, window, offsets):
+            nc.vector.tensor_copy(dst, window.indirect(offsets))
+
+        vg = [sb("vg%d" % a, [P, S], U32) for a in range(3)]
+        vg_sc = [sb("vg_sc%d" % a, [P, S], U8) for a in range(2)]
+        w1_q = [sb("w1_q%d" % h, [P, 512], U32) for h in range(2)]
+        w1_qs = [sb("w1_qs%d" % h, [P, 512], U8) for h in range(2)]
+
+        def quantize_w1(h):
+            grouped = sb("w1_bf%d" % h, [P, 2048], BF16)
+            nc.scalar.activation(
+                grouped[:].rearrange("p (t m j) -> p m t j", t=4, j=4),
+                w1_raw[h][:].rearrange("p j (m t) -> p m t j", t=4),
+                ACT.Copy,
+            )
+            nc.vector.quantize_mx(out=w1_q[h][:].bitcast(FP8X4), scales=w1_qs[h][:], in_=grouped[:])
+
+        gather(vg[0][:], v_words[0][:], list1[:])
+        gather(vg_sc[0][:], v_sc[:, 0, :], list1[:])
+        gather(vg_sc[1][:], v_sc[:, 1, :], list1[:])
+        quantize_w1(0)
+        v2g_sc = sb("v2g_sc", [P, S2], U8)
+        v3g_sc = sb("v3g_sc", [P, S2], U8)
+        gather(v2g_sc[:], v2_sc[:], list2[:])
+        gather(vg[1][:], v_words[1][:], list1[:])
+        gather(v3g_sc[:], v3_sc[:], list3[:])
+        quantize_w1(1)
+
+        def bank(jh, q, role):
+            return psum.tile([P, 2, HALF], F32, name="%s%d%d" % (role, jh, q), tag="bank%d%d" % (jh, q))
+
+        x = [[bank(jh, q, "x") for q in range(4)] for jh in range(2)]
+
+        def x_pass(a, jh):
+            js = slice(jh * HALF, (jh + 1) * HALF)
+            for c in range(8):
+                h, t = divmod(c, 4)
+                if a < 2:
+                    lhsT = w4_deal[:, a, 256 * c : 256 * (c + 1)].bitcast(FP4X4)
+                    lhsT_scale = w4_sc_deal[:, a, P * c : P * (c + 1)]
+                    rhs_scale = vg_sc[a][:, js]
+                else:
+                    lhsT = w1_q[h][:, P * t : P * (t + 1)].bitcast(FP8X4)
+                    lhsT_scale = w1_qs[h][:, P * t : P * (t + 1)]
+                    rhs_scale = vg_sc[1][V_K:P, js]
+                nc.tensor.matmul_mx(
+                    out=x[jh][c // 2][:, c % 2, :], lhsT=lhsT, lhsT_scale=lhsT_scale,
+                    rhs=vg[a][:, js].bitcast(FP8X4), rhs_scale=rhs_scale,
+                    start=(a == 0 and c % 2 == 0), stop=(a == 2 and c % 2 == 1),
+                )
+
+        for a in range(2):
+            for jh in range(2):
+                x_pass(a, jh)
+        for jh in range(2):
+            cols = slice(jh * LIST_COLS // 2, (jh + 1) * LIST_COLS // 2)
+            gather(vg[2][:, jh * HALF : (jh + 1) * HALF], v_words[2][:], list1[:, cols])
+            x_pass(2, jh)
+
+        h_q = {}
+        h_qs = {}
+
+        def make_h(jh, h):
+            mag = sb("mag%d%d" % (jh, h), [P, 4, HALF], F32)
+            for t in range(4):
+                nc.scalar.activation(
+                    mag[:, t, :], x[jh][2 * h + t // 2][:, t % 2, :], ACT.Abs, bias=b_sb[:, h, t : t + 1]
+                )
+            grouped = sb("h_bf%d%d" % (jh, h), [P, 4 * HALF], BF16)
+            nc.vector.tensor_tensor(
+                grouped[:].rearrange("p (c i t) -> p c t i", i=2, t=4),
+                mag[:].rearrange("p t (c i) -> p c t i", i=2),
+                g_sb[:, h, :].unsqueeze(1).unsqueeze(3).to_broadcast([P, HALF // 2, 4, 2]),
+                ALU.mult,
+            )
+            h_q[jh, h] = sb("h_q%d%d" % (jh, h), [P, HALF], U32)
+            h_qs[jh, h] = sb("h_qs%d%d" % (jh, h), [P, HALF], U8)
+            nc.vector.quantize_mx(out=h_q[jh, h][:].bitcast(FP8X4), scales=h_qs[jh, h][:], in_=grouped[:])
+
+        v2g = [sb("v2g%d" % a, [P, S2], U32) for a in range(2)]
+        v3g = [sb("v3g%d" % a, [P, S2], U32) for a in range(2)]
+
+        def e_pass(acc, words, scales, k, jh, mh, h):
+            for i in range(2):
+                ms = slice((2 * mh + i) * P, (2 * mh + i + 1) * P)
+                nc.tensor.matmul_mx(
+                    out=acc[:, i, :], lhsT=words[h][:, ms].bitcast(FP8X4), lhsT_scale=scales[k + 4 * h : P, ms],
+                    rhs=h_q[jh, h][:].bitcast(FP8X4), rhs_scale=h_qs[jh, h][:],
+                    start=(h == 0 and i == 0), stop=(h == 1 and i == 1),
+                )
+
+        sine = {}
+
+        def make_sine(jh, mh):
+            e2 = bank(jh, mh, "e2")
+            for h in range(2):
+                e_pass(e2, v2g, v2g_sc, V2_K, jh, mh, h)
+            turns = sb("turns%d%d" % (jh, mh), [P, 2 * HALF], F32)
+            whole = sb("whole%d%d" % (jh, mh), [P, 2 * HALF], U32)
+            rest = sb("rest%d%d" % (jh, mh), [P, 2 * HALF], F32)
+            sine[jh, mh] = sb("sine%d%d" % (jh, mh), [P, 2 * HALF], F32)
+            nc.scalar.activation(turns[:], e2[:].rearrange("p i j -> p (i j)"), ACT.Copy, scale=0.5 / math.pi)
+            nc.scalar.activation(whole[:], turns[:], ACT.Copy, bias=ROUNDER)
+            nc.vector.scalar_tensor_tensor(
+                rest[:], whole[:].bitcast(I32), ROUNDER, turns[:], ALU.subtract, ALU.subtract
+            )
+            nc.scalar.activation(sine[jh, mh][:], rest[:], ACT.Sin, scale=-2.0 * math.pi)
+
+        def finish(jh, mh, e3):
+            flat = e3[:].rearrange("p i j -> p (i j)")
+            mod = sb("mod%d%d" % (jh, mh), [P, 2 * HALF], F32)
+            best = sb("best%d%d" % (jh, mh), [P, 2 * HALF], F32)
+            res = sb("res%d%d" % (jh, mh), [P, 2, HALF], F32)
+            nc.vector.tensor_tensor(mod[:], flat, sine[jh, mh][:], ALU.mult)
+            nc.vector.tensor_tensor(best[:], flat, mod[:], ALU.max)
+            for i in range(2):
+                c = 2 * mh + i
+                nc.scalar.activation(
+                    res[:, i, :], best[:, i * HALF : (i + 1) * HALF], ACT.Copy, scale=w_sb[:, c : c + 1]
+                )
+            nc.sync.dma_start(
+                out[2 * P * mh : 2 * P * (mh + 1), jh * HALF : (jh + 1) * HALF].rearrange("(i p) j -> p i j", p=P),
+                res[:],
+            )
+
+        make_h(0, 0)
+        gather(v2g[0][:], v2_words[0][:], list2[:])
+        make_h(0, 1)
+        gather(v2g[1][:], v2_words[1][:], list2[:])
+        make_h(1, 0)
+        make_h(1, 1)
+        make_sine(0, 0)
+        make_sine(0, 1)
+        gather(v3g[0][:], v3_words[0][:], list3[:])
+        make_sine(1, 0)
+        make_sine(1, 1)
+        e3 = {}
+        for jh in range(2):
+            for mh in range(2):
+                e3[jh, mh] = bank(jh, 2 + mh, "e3")
+                e_pass(e3[jh, mh], v3g, v3g_sc, V3_K, jh, mh, 0)
+        for mh in range(2):
+            cols = slice(mh * LIST_COLS // 2, (mh + 1) * LIST_COLS // 2)
+            gather(v3g[1][:, mh * HALF : (mh + 1) * HALF], v3_words[1][:], list3[:, cols])
+            for jh in range(2):
+                e_pass(e3[jh, mh], v3g, v3g_sc, V3_K, jh, mh, 1)
+        for mh in range(2):
+            for jh in range(2):
+                finish(jh, mh, e3[jh, mh])

@@ -3,7 +3,7 @@ from contextlib import ExitStack
 
 import concourse.mybir as mybir
 
-K, KA, T, S, H, S2 = 1536, 1024, 2048, 512, 1024, 512
+K, T, S, H, S2 = 1536, 2048, 512, 1024, 512
 FLOPS = 2 * K * H * S + 2 * 2 * H * S2 * S
 
 F32 = mybir.dt.float32
@@ -18,9 +18,12 @@ ALU = mybir.AluOpType
 ACT = mybir.ActivationFunctionType
 
 P = 128
+PACK = 4
+PASS = P * PACK
 HALF = 256
 LIST_COLS = S // 16
 ROUNDER = 1.5 * 2.0**23
+V_PASS2_FIRST, V2_FIRST, V3_FIRST = 4, 8, 4
 
 
 def tile_list_islet_batch_scores_kernel(
@@ -35,6 +38,9 @@ def tile_list_islet_batch_scores_kernel(
         def sb(name, shape, dtype):
             return keep.tile(shape, dtype, name=name, align_bytes=64)
 
+        def sb_after(name, shape, dtype, tenant):
+            return keep.tile(shape, dtype, name=name, tag=tenant, align_bytes=64)
+
         list1 = keep.tile([P, LIST_COLS], U16, name="list1")
         list2 = keep.tile([P, LIST_COLS], U16, name="list2")
         list3 = keep.tile([P, LIST_COLS], U16, name="list3")
@@ -43,219 +49,233 @@ def tile_list_islet_batch_scores_kernel(
         v_sc = sb("v_sc", [P, 2, T], U8)
         v2_sc = sb("v2_sc", [P, T], U8)
         v3_sc = sb("v3_sc", [P, T], U8)
-        for plane in (w4_sc, v_sc, v2_sc, v3_sc):
-            nc.vector.memset(plane[:].bitcast(I32), 0)
+        nc.gpsimd.memset(w4_sc[:].bitcast(I32), 0)
+        nc.vector.memset(v_sc[:].bitcast(I32), 0)
+        nc.gpsimd.memset(v2_sc[:].bitcast(I32), 0)
+        nc.gpsimd.memset(v3_sc[:].bitcast(I32), 0)
 
         def load_words(name, words):
             tile = sb(name, [P, T], U32)
             nc.sync.dma_start(tile[:].bitcast(I32), words.rearrange("p n t -> p (n t)").bitcast(I32))
             return tile
 
-        def load_w1(h):
-            tile = sb("w1_raw%d" % h, [P, 4, 512], F32)
-            nc.sync.dma_start(tile[:], w1[:, 512 * h : 512 * (h + 1)].rearrange("(p j) c -> p j c", j=4))
+        def load_w1(col0, width):
+            tile = sb("w1_raw%d" % col0, [P, PACK, width], F32)
+            nc.sync.dma_start(tile[:], w1[:, col0 : col0 + width].rearrange("(p i) c -> p i c", i=PACK))
             return tile
 
-        nc.sync.dma_start(list1[:], offs)
-        for q in range(4):
-            nc.scalar.dma_start(
-                w4_sc[32 * q : 32 * q + 4, :, :].bitcast(I32),
-                w4_scales[:, 4 * q : 4 * q + 4, :].rearrange("a r n -> r a n").bitcast(I32),
-            )
-        w4_raw = sb("w4_raw", [P, 2, 2 * H], U8)
-        nc.sync.dma_start(w4_raw[:].bitcast(I32), w4_words.rearrange("a p n -> p a n").bitcast(I32))
-        v_words = [load_words("v_words0", tab_words[0])]
-        w1_raw = [load_w1(0)]
-        for q in range(4):
-            nc.scalar.dma_start(
-                v_sc[32 * q : 32 * q + 4, :, :].bitcast(I32),
-                tab_scales[0:2, 4 * q : 4 * q + 4, :].rearrange("a r n -> r a n").bitcast(I32),
-            )
-        w1_raw.append(load_w1(1))
-        v_words.append(load_words("v_words1", tab_words[1]))
-        v_words.append(load_words("v_words2", tab_words[2]))
-        b_sb = sb("b_sb", [P, 2, 4], F32)
-        g_sb = sb("g_sb", [P, 2, 4], F32)
-        w_sb = sb("w_sb", [P, 4], F32)
-        nc.sync.dma_start(b_sb[:], b.rearrange("(h p t) -> p h t", h=2, t=4))
-        nc.sync.dma_start(g_sb[:], gain.rearrange("(h p t) -> p h t", h=2, t=4))
-        nc.sync.dma_start(list2[:], offs2)
-        nc.sync.dma_start(list3[:], offs3)
-        with nc.allow_non_contiguous_dma(reason="one row weight a partition"):
-            nc.sync.dma_start(w_sb[:], wrow.rearrange("(c p) -> p c", p=P))
-        v2_words = [load_words("v2_words%d" % a, tab2_words[a]) for a in range(2)]
-        v3_words = [load_words("v3_words%d" % a, tab3_words[a]) for a in range(2)]
-
-        V_K, V2_K, V3_K = 4, 8, 4
-        for q in range(4):
-            nc.gpsimd.dma_start(
-                v_sc[32 * q + V_K : 32 * q + V_K + 4, 1, :].bitcast(I32),
-                tab_scales[2, 4 * q : 4 * q + 4, :].bitcast(I32),
-            )
-        for plane, scales, k in ((v2_sc, tab2_scales, V2_K), (v3_sc, tab3_scales, V3_K)):
-            for q in range(4):
-                nc.gpsimd.dma_start(
-                    plane[32 * q + k : 32 * q + k + 8, :].bitcast(I32),
-                    scales[:, 4 * q : 4 * q + 4, :].bitcast(I32),
+        def load_side_by_side(planes, scales, first):
+            for row in range(4):
+                nc.sync.dma_start(
+                    planes[first + row : P : 32].bitcast(I32),
+                    scales[:, row:16:4, :].rearrange("a q n -> q a n").bitcast(I32),
                 )
 
-        w4_deal = sb("w4_deal", [P, 2, 2 * H], U8)
-        w4_sc_deal = sb("w4_sc_deal", [P, 2, H], U8)
+        def load_stacked(planes, scales, first):
+            for quad in range(4):
+                nc.sync.dma_start(
+                    planes[32 * quad + first : 32 * quad + first + 8, :].bitcast(I32),
+                    scales[:, 4 * quad : 4 * quad + 4, :].bitcast(I32),
+                )
+
+        w4_raw = sb("w4_raw", [P, 2, 2 * H], U8)
+        b_sb = sb("b_sb", [P, 2, PACK], F32)
+        gain_sb = sb("gain_sb", [P, 2, PACK], F32)
+        wrow_sb = sb("wrow_sb", [P, S2 // P], F32)
+        nc.sync.dma_start(list1[:], offs)
+        nc.sync.dma_start(w4_raw[:].bitcast(I32), w4_words.rearrange("a p n -> p a n").bitcast(I32))
+        load_side_by_side(w4_sc[:], w4_scales, 0)
+        v_words = [load_words("v_words0", tab_words[0])]
+        load_side_by_side(v_sc[:], tab_scales[0:2], 0)
+        w1_raw = [[load_w1(0, PASS)]]
+        load_side_by_side(v_sc[:, 1:2, :], tab_scales[2:3], V_PASS2_FIRST)
+        v_words.append(load_words("v_words1", tab_words[1]))
+        nc.sync.dma_start(list2[:], offs2)
+        nc.sync.dma_start(b_sb[:], b.rearrange("(g p t) -> p g t", g=2, t=PACK))
+        nc.sync.dma_start(gain_sb[:], gain.rearrange("(g p t) -> p g t", g=2, t=PACK))
+        w1_raw.append([load_w1(PASS, PASS // 2), load_w1(PASS + PASS // 2, PASS // 2)])
+        v_words.append(load_words("v_words2", tab_words[2]))
+        load_stacked(v2_sc, tab2_scales, V2_FIRST)
+        v2_words = [load_words("v2_words%d" % g, tab2_words[g]) for g in range(2)]
+        nc.sync.dma_start(list3[:], offs3)
+        load_stacked(v3_sc, tab3_scales, V3_FIRST)
+        v3_words = [load_words("v3_words%d" % g, tab3_words[g]) for g in range(2)]
+        with nc.allow_non_contiguous_dma(reason="one row weight a partition"):
+            nc.sync.dma_start(wrow_sb[:], wrow.rearrange("(c p) -> p c", p=P))
+
+        w4_dealt = sb("w4_dealt", [P, 2, 2 * H], U8)
+        w4_sc_dealt = sb("w4_sc_dealt", [P, 2, H], U8)
         nc.vector.tensor_copy(
-            w4_deal[:].bitcast(U16).rearrange("p a (h t m) -> p (a h) t m", h=2, t=4),
-            w4_raw[:].bitcast(U16).rearrange("p a (h m t) -> p (a h) t m", h=2, t=4),
+            w4_dealt[:].bitcast(U16).rearrange("p a (g t c) -> p (a g) t c", g=2, t=PACK),
+            w4_raw[:].bitcast(U16).rearrange("p a (g c t) -> p (a g) t c", g=2, t=PACK),
         )
         nc.vector.tensor_copy(
-            w4_sc_deal[:].rearrange("p a (h t m) -> p (a h) t m", h=2, t=4),
-            w4_sc[:].rearrange("p a (h m t) -> p (a h) t m", h=2, t=4),
+            w4_sc_dealt[:].rearrange("p a (g t c) -> p (a g) t c", g=2, t=PACK),
+            w4_sc[:].rearrange("p a (g c t) -> p (a g) t c", g=2, t=PACK),
         )
 
         def gather(dst, window, offsets):
             nc.vector.tensor_copy(dst, window.indirect(offsets))
 
+        def list_half(tile, half):
+            return tile[:, half * LIST_COLS // 2 : (half + 1) * LIST_COLS // 2]
+
         vg = [sb("vg%d" % a, [P, S], U32) for a in range(3)]
-        vg_sc = [sb("vg_sc%d" % a, [P, S], U8) for a in range(2)]
-        w1_q = [sb("w1_q%d" % h, [P, 512], U32) for h in range(2)]
-        w1_qs = [sb("w1_qs%d" % h, [P, 512], U8) for h in range(2)]
+        vg_sc = [sb("vg_sc%d" % n, [P, S], U8) for n in range(2)]
+        w1_q = [sb("w1_q%d" % g, [P, PASS], U32) for g in range(2)]
+        w1_q_sc = [sb("w1_q_sc%d" % g, [P, PASS], U8) for g in range(2)]
 
-        def quantize_w1(h):
-            grouped = sb("w1_bf%d" % h, [P, 2048], BF16)
-            nc.scalar.activation(
-                grouped[:].rearrange("p (t m j) -> p m t j", t=4, j=4),
-                w1_raw[h][:].rearrange("p j (m t) -> p m t j", t=4),
-                ACT.Copy,
-            )
-            nc.vector.quantize_mx(out=w1_q[h][:].bitcast(FP8X4), scales=w1_qs[h][:], in_=grouped[:])
+        def quantize_w1(g):
+            rounded = sb("w1_bf%d" % g, [P, PACK * PASS], BF16)
+            dealt = rounded[:].rearrange("p (t c i) -> p c t i", t=PACK, i=PACK)
+            width = P // len(w1_raw[g])
+            for n, raw in enumerate(w1_raw[g]):
+                nc.scalar.activation(
+                    dealt[:, n * width : (n + 1) * width], raw[:].rearrange("p i (c t) -> p c t i", t=PACK), ACT.Copy
+                )
+            nc.vector.quantize_mx(out=w1_q[g][:].bitcast(FP8X4), scales=w1_q_sc[g][:], in_=rounded[:])
 
-        gather(vg[0][:], v_words[0][:], list1[:])
-        gather(vg_sc[0][:], v_sc[:, 0, :], list1[:])
-        gather(vg_sc[1][:], v_sc[:, 1, :], list1[:])
-        quantize_w1(0)
         v2g_sc = sb("v2g_sc", [P, S2], U8)
         v3g_sc = sb("v3g_sc", [P, S2], U8)
-        gather(v2g_sc[:], v2_sc[:], list2[:])
+        gather(vg[0][:], v_words[0][:], list1[:])
+        for n in range(2):
+            gather(vg_sc[n][:], v_sc[:, n, :], list1[:])
+        quantize_w1(0)
         gather(vg[1][:], v_words[1][:], list1[:])
-        gather(v3g_sc[:], v3_sc[:], list3[:])
         quantize_w1(1)
 
-        def bank(jh, q, role):
-            return psum.tile([P, 2, HALF], F32, name="%s%d%d" % (role, jh, q), tag="bank%d%d" % (jh, q))
+        gain_b = sb("gain_b", [P, 2, PACK], F32)
+        gain_sign = sb("gain_sign", [P, 2, PACK], BF16)
+        nc.vector.tensor_tensor(gain_b[:], gain_sb[:], b_sb[:], ALU.mult)
+        nc.scalar.activation(gain_sign[:], gain_sb[:], ACT.Sign)
 
-        x = [[bank(jh, q, "x") for q in range(4)] for jh in range(2)]
+        def bank(role, jh, n):
+            return psum.tile([P, 2, HALF], F32, name="%s%d%d" % (role, jh, n), tag="bank%d%d" % (jh, n))
+
+        x = [[bank("x", jh, n) for n in range(4)] for jh in range(2)]
 
         def x_pass(a, jh):
             js = slice(jh * HALF, (jh + 1) * HALF)
-            for c in range(8):
-                h, t = divmod(c, 4)
+            for s in range(2 * PACK):
+                g, t = divmod(s, PACK)
                 if a < 2:
-                    lhsT = w4_deal[:, a, 256 * c : 256 * (c + 1)].bitcast(FP4X4)
-                    lhsT_scale = w4_sc_deal[:, a, P * c : P * (c + 1)]
+                    lhsT = w4_dealt[:, a, 2 * P * s : 2 * P * (s + 1)].bitcast(FP4X4)
+                    lhsT_scale = w4_sc_dealt[:, a, P * s : P * (s + 1)]
                     rhs_scale = vg_sc[a][:, js]
                 else:
-                    lhsT = w1_q[h][:, P * t : P * (t + 1)].bitcast(FP8X4)
-                    lhsT_scale = w1_qs[h][:, P * t : P * (t + 1)]
-                    rhs_scale = vg_sc[1][V_K:P, js]
+                    lhsT = w1_q[g][:, P * t : P * (t + 1)].bitcast(FP8X4)
+                    lhsT_scale = w1_q_sc[g][:, P * t : P * (t + 1)]
+                    rhs_scale = vg_sc[1][V_PASS2_FIRST:P, js]
                 nc.tensor.matmul_mx(
-                    out=x[jh][c // 2][:, c % 2, :], lhsT=lhsT, lhsT_scale=lhsT_scale,
+                    out=x[jh][s // 2][:, s % 2, :], lhsT=lhsT, lhsT_scale=lhsT_scale,
                     rhs=vg[a][:, js].bitcast(FP8X4), rhs_scale=rhs_scale,
-                    start=(a == 0 and c % 2 == 0), stop=(a == 2 and c % 2 == 1),
+                    start=(a == 0 and s % 2 == 0), stop=(a == 2 and s % 2 == 1),
                 )
 
         for a in range(2):
             for jh in range(2):
                 x_pass(a, jh)
         for jh in range(2):
-            cols = slice(jh * LIST_COLS // 2, (jh + 1) * LIST_COLS // 2)
-            gather(vg[2][:, jh * HALF : (jh + 1) * HALF], v_words[2][:], list1[:, cols])
+            gather(vg[2][:, jh * HALF : (jh + 1) * HALF], v_words[2][:], list_half(list1, jh))
             x_pass(2, jh)
 
         h_q = {}
-        h_qs = {}
+        h_q_sc = {}
 
-        def make_h(jh, h):
-            mag = sb("mag%d%d" % (jh, h), [P, 4, HALF], F32)
-            for t in range(4):
+        def make_h(jh, g, tenant):
+            pairs = sb("pairs%d%d" % (jh, g), [P, 2, HALF, 2], BF16)
+            for t in range(PACK):
                 nc.scalar.activation(
-                    mag[:, t, :], x[jh][2 * h + t // 2][:, t % 2, :], ACT.Abs, bias=b_sb[:, h, t : t + 1]
+                    pairs[:, t // 2, :, t % 2], x[jh][2 * g + t // 2][:, t % 2, :], ACT.Abs,
+                    scale=gain_sb[:, g, t : t + 1], bias=gain_b[:, g, t : t + 1],
                 )
-            grouped = sb("h_bf%d%d" % (jh, h), [P, 4 * HALF], BF16)
+            signed = sb_after("h_bf%d%d" % (jh, g), [P, PACK * HALF], BF16, tenant)
             nc.vector.tensor_tensor(
-                grouped[:].rearrange("p (c i t) -> p c t i", i=2, t=4),
-                mag[:].rearrange("p t (c i) -> p c t i", i=2),
-                g_sb[:, h, :].unsqueeze(1).unsqueeze(3).to_broadcast([P, HALF // 2, 4, 2]),
+                signed[:].rearrange("p (j u e) -> p j u e", u=2, e=2),
+                pairs[:].rearrange("p u j e -> p j u e"),
+                gain_sign[:, g, :].rearrange("p (u e) -> p u e", e=2).unsqueeze(1).to_broadcast([P, HALF, 2, 2]),
                 ALU.mult,
             )
-            h_q[jh, h] = sb("h_q%d%d" % (jh, h), [P, HALF], U32)
-            h_qs[jh, h] = sb("h_qs%d%d" % (jh, h), [P, HALF], U8)
-            nc.vector.quantize_mx(out=h_q[jh, h][:].bitcast(FP8X4), scales=h_qs[jh, h][:], in_=grouped[:])
+            h_q[jh, g] = sb("h_q%d%d" % (jh, g), [P, HALF], U32)
+            h_q_sc[jh, g] = sb("h_q_sc%d%d" % (jh, g), [P, HALF], U8)
+            nc.vector.quantize_mx(out=h_q[jh, g][:].bitcast(FP8X4), scales=h_q_sc[jh, g][:], in_=signed[:])
 
-        v2g = [sb("v2g%d" % a, [P, S2], U32) for a in range(2)]
-        v3g = [sb("v3g%d" % a, [P, S2], U32) for a in range(2)]
+        v2g = [sb("v2g%d" % g, [P, S2], U32) for g in range(2)]
+        v3g = [sb("v3g%d" % g, [P, S2], U32) for g in range(2)]
 
-        def e_pass(acc, words, scales, k, jh, mh, h):
+        def e_pass(acc, words, planes, first, jh, mh, g):
             for i in range(2):
                 ms = slice((2 * mh + i) * P, (2 * mh + i + 1) * P)
                 nc.tensor.matmul_mx(
-                    out=acc[:, i, :], lhsT=words[h][:, ms].bitcast(FP8X4), lhsT_scale=scales[k + 4 * h : P, ms],
-                    rhs=h_q[jh, h][:].bitcast(FP8X4), rhs_scale=h_qs[jh, h][:],
-                    start=(h == 0 and i == 0), stop=(h == 1 and i == 1),
+                    out=acc[:, i, :], lhsT=words[g][:, ms].bitcast(FP8X4), lhsT_scale=planes[first + 4 * g : P, ms],
+                    rhs=h_q[jh, g][:].bitcast(FP8X4), rhs_scale=h_q_sc[jh, g][:],
+                    start=(g == 0 and i == 0), stop=(g == 1 and i == 1),
                 )
 
         sine = {}
 
-        def make_sine(jh, mh):
-            e2 = bank(jh, mh, "e2")
-            for h in range(2):
-                e_pass(e2, v2g, v2g_sc, V2_K, jh, mh, h)
+        def make_sine(jh, mh, rest):
+            e2 = bank("e2", jh, mh)
+            for g in range(2):
+                e_pass(e2, v2g, v2g_sc, V2_FIRST, jh, mh, g)
             turns = sb("turns%d%d" % (jh, mh), [P, 2 * HALF], F32)
             whole = sb("whole%d%d" % (jh, mh), [P, 2 * HALF], U32)
-            rest = sb("rest%d%d" % (jh, mh), [P, 2 * HALF], F32)
             sine[jh, mh] = sb("sine%d%d" % (jh, mh), [P, 2 * HALF], F32)
             nc.scalar.activation(turns[:], e2[:].rearrange("p i j -> p (i j)"), ACT.Copy, scale=0.5 / math.pi)
             nc.scalar.activation(whole[:], turns[:], ACT.Copy, bias=ROUNDER)
-            nc.vector.scalar_tensor_tensor(
-                rest[:], whole[:].bitcast(I32), ROUNDER, turns[:], ALU.subtract, ALU.subtract
-            )
-            nc.scalar.activation(sine[jh, mh][:], rest[:], ACT.Sin, scale=-2.0 * math.pi)
+            nc.vector.scalar_tensor_tensor(rest, whole[:].bitcast(I32), ROUNDER, turns[:], ALU.subtract, ALU.subtract)
+            nc.scalar.activation(sine[jh, mh][:], rest, ACT.Sin, scale=-2.0 * math.pi)
 
-        def finish(jh, mh, e3):
-            flat = e3[:].rearrange("p i j -> p (i j)")
-            mod = sb("mod%d%d" % (jh, mh), [P, 2 * HALF], F32)
-            best = sb("best%d%d" % (jh, mh), [P, 2 * HALF], F32)
-            res = sb("res%d%d" % (jh, mh), [P, 2, HALF], F32)
-            nc.vector.tensor_tensor(mod[:], flat, sine[jh, mh][:], ALU.mult)
-            nc.vector.tensor_tensor(best[:], flat, mod[:], ALU.max)
-            for i in range(2):
-                c = 2 * mh + i
-                nc.scalar.activation(
-                    res[:, i, :], best[:, i * HALF : (i + 1) * HALF], ACT.Copy, scale=w_sb[:, c : c + 1]
-                )
-            nc.sync.dma_start(
-                out[2 * P * mh : 2 * P * (mh + 1), jh * HALF : (jh + 1) * HALF].rearrange("(i p) j -> p i j", p=P),
-                res[:],
-            )
-
-        make_h(0, 0)
-        gather(v2g[0][:], v2_words[0][:], list2[:])
-        make_h(0, 1)
-        gather(v2g[1][:], v2_words[1][:], list2[:])
-        make_h(1, 0)
-        make_h(1, 1)
-        make_sine(0, 0)
-        make_sine(0, 1)
-        gather(v3g[0][:], v3_words[0][:], list3[:])
-        make_sine(1, 0)
-        make_sine(1, 1)
         e3 = {}
+
+        def finish(jh, mh, tiles, weigh_on_vector):
+            name = "%d%d%d" % (jh, mh, tiles[0])
+            cols = slice(tiles[0] * HALF, (tiles[-1] + 1) * HALF)
+            score = e3[jh, mh][:].rearrange("p i j -> p (i j)")[:, cols]
+            modulated = sb("modulated" + name, [P, len(tiles) * HALF], F32)
+            best = sb("best" + name, [P, len(tiles) * HALF], F32)
+            result = sb("result" + name, [P, len(tiles), HALF], F32)
+            nc.vector.tensor_tensor(modulated[:], score, sine[jh, mh][:, cols], ALU.mult)
+            nc.vector.tensor_tensor(best[:], score, modulated[:], ALU.max)
+            for n, i in enumerate(tiles):
+                weight = wrow_sb[:, 2 * mh + i : 2 * mh + i + 1]
+                if weigh_on_vector:
+                    nc.vector.tensor_scalar(result[:, n, :], best[:, n * HALF : (n + 1) * HALF], weight, None, ALU.mult)
+                else:
+                    nc.scalar.activation(result[:, n, :], best[:, n * HALF : (n + 1) * HALF], ACT.Copy, scale=weight)
+            row0 = (2 * mh + tiles[0]) * P
+            nc.sync.dma_start(
+                out[row0 : row0 + len(tiles) * P, jh * HALF : (jh + 1) * HALF].rearrange("(i p) j -> p i j", p=P),
+                result[:],
+            )
+
+        gather(v2g_sc[:], v2_sc[:], list2[:])
+        make_h(0, 0, "v2_sc")
+        gather(v2g[0][:], v2_words[0][:], list2[:])
+        make_h(0, 1, "v2_words0")
+        gather(v2g[1][:], v2_words[1][:], list2[:])
+        make_h(1, 0, "v2_words1")
+        gather(v3g_sc[:], v3_sc[:], list3[:])
+        make_h(1, 1, "v3_sc")
+        gather(v3g[0][:], v3_words[0][:], list3[:])
+
         for jh in range(2):
             for mh in range(2):
-                e3[jh, mh] = bank(jh, 2 + mh, "e3")
-                e_pass(e3[jh, mh], v3g, v3g_sc, V3_K, jh, mh, 0)
+                e3[jh, mh] = bank("e3", jh, 2 + mh)
+        first_rest = sb_after("first_rest", [P, 2 * HALF], F32, "v3_words0")
+        make_sine(0, 0, first_rest[:])
+        for jh in range(2):
+            for mh in range(2):
+                e_pass(e3[jh, mh], v3g, v3g_sc, V3_FIRST, jh, mh, 0)
         for mh in range(2):
-            cols = slice(mh * LIST_COLS // 2, (mh + 1) * LIST_COLS // 2)
-            gather(v3g[1][:, mh * HALF : (mh + 1) * HALF], v3_words[1][:], list3[:, cols])
+            gather(v3g[1][:, mh * HALF : (mh + 1) * HALF], v3_words[1][:], list_half(list3, mh))
             for jh in range(2):
-                e_pass(e3[jh, mh], v3g, v3g_sc, V3_K, jh, mh, 1)
-        for mh in range(2):
-            for jh in range(2):
-                finish(jh, mh, e3[jh, mh])
+                e_pass(e3[jh, mh], v3g, v3g_sc, V3_FIRST, jh, mh, 1)
+        later_rests = sb_after("later_rests", [P, 3, 2 * HALF], F32, "v3_words1")
+        for n, (jh, mh) in enumerate(((0, 1), (1, 0), (1, 1))):
+            make_sine(jh, mh, later_rests[:, n, :])
+
+        for jh, mh in ((0, 0), (0, 1), (1, 0)):
+            finish(jh, mh, (0, 1), False)
+        finish(1, 1, (0,), False)
+        finish(1, 1, (1,), True)

import math
from contextlib import ExitStack

import concourse.mybir as mybir

K, T, S, H, S2 = 1536, 2048, 512, 1024, 512
FLOPS = 2 * K * H * S + 2 * 2 * H * S2 * S

F32 = mybir.dt.float32
BF16 = mybir.dt.bfloat16
I32 = mybir.dt.int32
U32 = mybir.dt.uint32
U16 = mybir.dt.uint16
U8 = mybir.dt.uint8
FP8X4 = mybir.dt.float8_e4m3fn_x4
FP4X4 = mybir.dt.float4_e2m1fn_x4
ALU = mybir.AluOpType
ACT = mybir.ActivationFunctionType

P = 128
PACK = 4
PASS = P * PACK
HALF = 256
LIST_COLS = S // 16
ROUNDER = 1.5 * 2.0**23
V_PASS2_FIRST, V2_FIRST, V3_FIRST = 4, 8, 4


def tile_list_islet_batch_scores_kernel(
    tc, tab_words, tab_scales, offs, tab2_words, tab2_scales, offs2, tab3_words, tab3_scales, offs3,
    w4_words, w4_scales, w1, b, gain, wrow, out,
):
    nc = tc.nc
    with ExitStack() as ctx:
        keep = ctx.enter_context(tc.tile_pool(name="keep", bufs=1))
        psum = ctx.enter_context(tc.psum_pool(name="psum", bufs=1))

        def sb(name, shape, dtype):
            return keep.tile(shape, dtype, name=name, align_bytes=64)

        def sb_after(name, shape, dtype, tenant):
            return keep.tile(shape, dtype, name=name, tag=tenant, align_bytes=64)

        list1 = keep.tile([P, LIST_COLS], U16, name="list1")
        list2 = keep.tile([P, LIST_COLS], U16, name="list2")
        list3 = keep.tile([P, LIST_COLS], U16, name="list3")

        w4_sc = sb("w4_sc", [P, 2, H], U8)
        v_sc = sb("v_sc", [P, 2, T], U8)
        v2_sc = sb("v2_sc", [P, T], U8)
        v3_sc = sb("v3_sc", [P, T], U8)
        nc.gpsimd.memset(w4_sc[:].bitcast(I32), 0)
        nc.vector.memset(v_sc[:].bitcast(I32), 0)
        nc.gpsimd.memset(v2_sc[:].bitcast(I32), 0)
        nc.gpsimd.memset(v3_sc[:].bitcast(I32), 0)

        def load_words(name, words):
            tile = sb(name, [P, T], U32)
            nc.sync.dma_start(tile[:].bitcast(I32), words.rearrange("p n t -> p (n t)").bitcast(I32))
            return tile

        def load_w1(col0, width):
            tile = sb("w1_raw%d" % col0, [P, PACK, width], F32)
            nc.sync.dma_start(tile[:], w1[:, col0 : col0 + width].rearrange("(p i) c -> p i c", i=PACK))
            return tile

        def load_side_by_side(planes, scales, first):
            for row in range(4):
                nc.sync.dma_start(
                    planes[first + row : P : 32].bitcast(I32),
                    scales[:, row:16:4, :].rearrange("a q n -> q a n").bitcast(I32),
                )

        def load_stacked(planes, scales, first):
            for quad in range(4):
                nc.sync.dma_start(
                    planes[32 * quad + first : 32 * quad + first + 8, :].bitcast(I32),
                    scales[:, 4 * quad : 4 * quad + 4, :].bitcast(I32),
                )

        w4_raw = sb("w4_raw", [P, 2, 2 * H], U8)
        b_sb = sb("b_sb", [P, 2, PACK], F32)
        gain_sb = sb("gain_sb", [P, 2, PACK], F32)
        wrow_sb = sb("wrow_sb", [P, S2 // P], F32)
        nc.sync.dma_start(list1[:], offs)
        nc.sync.dma_start(w4_raw[:].bitcast(I32), w4_words.rearrange("a p n -> p a n").bitcast(I32))
        load_side_by_side(w4_sc[:], w4_scales, 0)
        v_words = [load_words("v_words0", tab_words[0])]
        load_side_by_side(v_sc[:], tab_scales[0:2], 0)
        w1_raw = [[load_w1(0, PASS)]]
        load_side_by_side(v_sc[:, 1:2, :], tab_scales[2:3], V_PASS2_FIRST)
        v_words.append(load_words("v_words1", tab_words[1]))
        nc.sync.dma_start(list2[:], offs2)
        nc.sync.dma_start(b_sb[:], b.rearrange("(g p t) -> p g t", g=2, t=PACK))
        nc.sync.dma_start(gain_sb[:], gain.rearrange("(g p t) -> p g t", g=2, t=PACK))
        w1_raw.append([load_w1(PASS, PASS // 2), load_w1(PASS + PASS // 2, PASS // 2)])
        v_words.append(load_words("v_words2", tab_words[2]))
        load_stacked(v2_sc, tab2_scales, V2_FIRST)
        v2_words = [load_words("v2_words%d" % g, tab2_words[g]) for g in range(2)]
        nc.sync.dma_start(list3[:], offs3)
        load_stacked(v3_sc, tab3_scales, V3_FIRST)
        v3_words = [load_words("v3_words%d" % g, tab3_words[g]) for g in range(2)]
        with nc.allow_non_contiguous_dma(reason="one row weight a partition"):
            nc.sync.dma_start(wrow_sb[:], wrow.rearrange("(c p) -> p c", p=P))

        w4_dealt = sb("w4_dealt", [P, 2, 2 * H], U8)
        w4_sc_dealt = sb("w4_sc_dealt", [P, 2, H], U8)
        nc.vector.tensor_copy(
            w4_dealt[:].bitcast(U16).rearrange("p a (g t c) -> p (a g) t c", g=2, t=PACK),
            w4_raw[:].bitcast(U16).rearrange("p a (g c t) -> p (a g) t c", g=2, t=PACK),
        )
        nc.vector.tensor_copy(
            w4_sc_dealt[:].rearrange("p a (g t c) -> p (a g) t c", g=2, t=PACK),
            w4_sc[:].rearrange("p a (g c t) -> p (a g) t c", g=2, t=PACK),
        )

        def gather(dst, window, offsets):
            nc.vector.tensor_copy(dst, window.indirect(offsets))

        def list_half(tile, half):
            return tile[:, half * LIST_COLS // 2 : (half + 1) * LIST_COLS // 2]

        vg = [sb("vg%d" % a, [P, S], U32) for a in range(3)]
        vg_sc = [sb("vg_sc%d" % n, [P, S], U8) for n in range(2)]
        w1_q = [sb("w1_q%d" % g, [P, PASS], U32) for g in range(2)]
        w1_q_sc = [sb("w1_q_sc%d" % g, [P, PASS], U8) for g in range(2)]

        def quantize_w1(g):
            rounded = sb("w1_bf%d" % g, [P, PACK * PASS], BF16)
            dealt = rounded[:].rearrange("p (t c i) -> p c t i", t=PACK, i=PACK)
            width = P // len(w1_raw[g])
            for n, raw in enumerate(w1_raw[g]):
                nc.scalar.activation(
                    dealt[:, n * width : (n + 1) * width], raw[:].rearrange("p i (c t) -> p c t i", t=PACK), ACT.Copy
                )
            nc.vector.quantize_mx(out=w1_q[g][:].bitcast(FP8X4), scales=w1_q_sc[g][:], in_=rounded[:])

        v2g_sc = sb("v2g_sc", [P, S2], U8)
        v3g_sc = sb("v3g_sc", [P, S2], U8)
        gather(vg[0][:], v_words[0][:], list1[:])
        for n in range(2):
            gather(vg_sc[n][:], v_sc[:, n, :], list1[:])
        quantize_w1(0)
        gather(vg[1][:], v_words[1][:], list1[:])
        quantize_w1(1)

        gain_b = sb("gain_b", [P, 2, PACK], F32)
        gain_sign = sb("gain_sign", [P, 2, PACK], BF16)
        nc.vector.tensor_tensor(gain_b[:], gain_sb[:], b_sb[:], ALU.mult)
        nc.scalar.activation(gain_sign[:], gain_sb[:], ACT.Sign)

        def bank(role, jh, n):
            return psum.tile([P, 2, HALF], F32, name="%s%d%d" % (role, jh, n), tag="bank%d%d" % (jh, n))

        x = [[bank("x", jh, n) for n in range(4)] for jh in range(2)]

        def x_pass(a, jh):
            js = slice(jh * HALF, (jh + 1) * HALF)
            for s in range(2 * PACK):
                g, t = divmod(s, PACK)
                if a < 2:
                    lhsT = w4_dealt[:, a, 2 * P * s : 2 * P * (s + 1)].bitcast(FP4X4)
                    lhsT_scale = w4_sc_dealt[:, a, P * s : P * (s + 1)]
                    rhs_scale = vg_sc[a][:, js]
                else:
                    lhsT = w1_q[g][:, P * t : P * (t + 1)].bitcast(FP8X4)
                    lhsT_scale = w1_q_sc[g][:, P * t : P * (t + 1)]
                    rhs_scale = vg_sc[1][V_PASS2_FIRST:P, js]
                nc.tensor.matmul_mx(
                    out=x[jh][s // 2][:, s % 2, :], lhsT=lhsT, lhsT_scale=lhsT_scale,
                    rhs=vg[a][:, js].bitcast(FP8X4), rhs_scale=rhs_scale,
                    start=(a == 0 and s % 2 == 0), stop=(a == 2 and s % 2 == 1),
                )

        for a in range(2):
            for jh in range(2):
                x_pass(a, jh)
        for jh in range(2):
            gather(vg[2][:, jh * HALF : (jh + 1) * HALF], v_words[2][:], list_half(list1, jh))
            x_pass(2, jh)

        h_q = {}
        h_q_sc = {}

        def make_h(jh, g, tenant):
            pairs = sb("pairs%d%d" % (jh, g), [P, 2, HALF, 2], BF16)
            for t in range(PACK):
                nc.scalar.activation(
                    pairs[:, t // 2, :, t % 2], x[jh][2 * g + t // 2][:, t % 2, :], ACT.Abs,
                    scale=gain_sb[:, g, t : t + 1], bias=gain_b[:, g, t : t + 1],
                )
            signed = sb_after("h_bf%d%d" % (jh, g), [P, PACK * HALF], BF16, tenant)
            nc.vector.tensor_tensor(
                signed[:].rearrange("p (j u e) -> p j u e", u=2, e=2),
                pairs[:].rearrange("p u j e -> p j u e"),
                gain_sign[:, g, :].rearrange("p (u e) -> p u e", e=2).unsqueeze(1).to_broadcast([P, HALF, 2, 2]),
                ALU.mult,
            )
            h_q[jh, g] = sb("h_q%d%d" % (jh, g), [P, HALF], U32)
            h_q_sc[jh, g] = sb("h_q_sc%d%d" % (jh, g), [P, HALF], U8)
            nc.vector.quantize_mx(out=h_q[jh, g][:].bitcast(FP8X4), scales=h_q_sc[jh, g][:], in_=signed[:])

        v2g = [sb("v2g%d" % g, [P, S2], U32) for g in range(2)]
        v3g = [sb("v3g%d" % g, [P, S2], U32) for g in range(2)]

        def e_pass(acc, words, planes, first, jh, mh, g):
            for i in range(2):
                ms = slice((2 * mh + i) * P, (2 * mh + i + 1) * P)
                nc.tensor.matmul_mx(
                    out=acc[:, i, :], lhsT=words[g][:, ms].bitcast(FP8X4), lhsT_scale=planes[first + 4 * g : P, ms],
                    rhs=h_q[jh, g][:].bitcast(FP8X4), rhs_scale=h_q_sc[jh, g][:],
                    start=(g == 0 and i == 0), stop=(g == 1 and i == 1),
                )

        sine = {}

        def make_sine(jh, mh, rest):
            e2 = bank("e2", jh, mh)
            for g in range(2):
                e_pass(e2, v2g, v2g_sc, V2_FIRST, jh, mh, g)
            turns = sb("turns%d%d" % (jh, mh), [P, 2 * HALF], F32)
            whole = sb("whole%d%d" % (jh, mh), [P, 2 * HALF], U32)
            sine[jh, mh] = sb("sine%d%d" % (jh, mh), [P, 2 * HALF], F32)
            nc.scalar.activation(turns[:], e2[:].rearrange("p i j -> p (i j)"), ACT.Copy, scale=0.5 / math.pi)
            nc.scalar.activation(whole[:], turns[:], ACT.Copy, bias=ROUNDER)
            nc.vector.scalar_tensor_tensor(rest, whole[:].bitcast(I32), ROUNDER, turns[:], ALU.subtract, ALU.subtract)
            nc.scalar.activation(sine[jh, mh][:], rest, ACT.Sin, scale=-2.0 * math.pi)

        e3 = {}

        def finish(jh, mh, tiles, weigh_on_vector):
            name = "%d%d%d" % (jh, mh, tiles[0])
            cols = slice(tiles[0] * HALF, (tiles[-1] + 1) * HALF)
            score = e3[jh, mh][:].rearrange("p i j -> p (i j)")[:, cols]
            modulated = sb("modulated" + name, [P, len(tiles) * HALF], F32)
            best = sb("best" + name, [P, len(tiles) * HALF], F32)
            result = sb("result" + name, [P, len(tiles), HALF], F32)
            nc.vector.tensor_tensor(modulated[:], score, sine[jh, mh][:, cols], ALU.mult)
            nc.vector.tensor_tensor(best[:], score, modulated[:], ALU.max)
            for n, i in enumerate(tiles):
                weight = wrow_sb[:, 2 * mh + i : 2 * mh + i + 1]
                if weigh_on_vector:
                    nc.vector.tensor_scalar(result[:, n, :], best[:, n * HALF : (n + 1) * HALF], weight, None, ALU.mult)
                else:
                    nc.scalar.activation(result[:, n, :], best[:, n * HALF : (n + 1) * HALF], ACT.Copy, scale=weight)
            row0 = (2 * mh + tiles[0]) * P
            nc.sync.dma_start(
                out[row0 : row0 + len(tiles) * P, jh * HALF : (jh + 1) * HALF].rearrange("(i p) j -> p i j", p=P),
                result[:],
            )

        gather(v2g_sc[:], v2_sc[:], list2[:])
        make_h(0, 0, "v2_sc")
        gather(v2g[0][:], v2_words[0][:], list2[:])
        make_h(0, 1, "v2_words0")
        gather(v2g[1][:], v2_words[1][:], list2[:])
        make_h(1, 0, "v2_words1")
        gather(v3g_sc[:], v3_sc[:], list3[:])
        make_h(1, 1, "v3_sc")
        gather(v3g[0][:], v3_words[0][:], list3[:])

        for jh in range(2):
            for mh in range(2):
                e3[jh, mh] = bank("e3", jh, 2 + mh)
        first_rest = sb_after("first_rest", [P, 2 * HALF], F32, "v3_words0")
        make_sine(0, 0, first_rest[:])
        for jh in range(2):
            for mh in range(2):
                e_pass(e3[jh, mh], v3g, v3g_sc, V3_FIRST, jh, mh, 0)
        for mh in range(2):
            gather(v3g[1][:, mh * HALF : (mh + 1) * HALF], v3_words[1][:], list_half(list3, mh))
            for jh in range(2):
                e_pass(e3[jh, mh], v3g, v3g_sc, V3_FIRST, jh, mh, 1)
        later_rests = sb_after("later_rests", [P, 3, 2 * HALF], F32, "v3_words1")
        for n, (jh, mh) in enumerate(((0, 1), (1, 0), (1, 1))):
            make_sine(jh, mh, later_rests[:, n, :])

        for jh, mh in ((0, 0), (0, 1), (1, 0)):
            finish(jh, mh, (0, 1), False)
        finish(1, 1, (0,), False)
        finish(1, 1, (1,), True)
